import numpy as np, ml_dtypes
CORES = [2,6,10,14,18,22,26,30]
N = 8
import mx_ref
BF = ml_dtypes.bfloat16
def gcols(t, e):
    v = np.concatenate([t.reshape(8, 16, -1, 4), np.zeros((8, 16, 1, 4), BF)], axis=2)
    return np.ascontiguousarray(np.stack([v[g][:, e[g]] for g in range(8)])).reshape(128, -1)
def tile(rs):
    return np.stack(rs, axis=2).reshape(128, -1).astype(BF)
def pick(q, e):
    c = np.concatenate([q[0].reshape(128, -1, 4), np.zeros((128, 1, 4), np.uint8)], axis=1); s = np.concatenate([q[1], np.ones((16, 1), np.uint8)], axis=1)
    return (np.ascontiguousarray(c[:, e].reshape(128, -1)), np.ascontiguousarray(s[:, e]))
def join(*qs):
    return (np.concatenate([q[0] for q in qs], axis=1), np.concatenate([q[1] for q in qs], axis=1))
def put(q, e, v):
    c, s = q[0].reshape(128, -1, 4).copy(), q[1].copy(); c[:, e] = v[0].reshape(128, -1, 4); s[:, e] = v[1]
    return (c.reshape(128, -1), s)
def pk(c, s):
    return (np.ascontiguousarray(c), mx_ref.live(s))
def emit(q):
    return q[0], q[1]
def packed(v, rng):
    q = [mx_ref.quantize(np.ascontiguousarray(v[r])) for r in range(N)]
    return np.stack([a for a, b in q]), np.stack([mx_ref.plane(b, rng) for a, b in q])
def values_of_codes():
    e, c = np.zeros((128, 128, 4), np.float32), np.zeros((128, 2, 4), np.uint8)
    e[np.arange(128), np.arange(128), 0] = 1
    c[:127, :, 0] = np.arange(256).reshape(2, 128).T[:127]
    return mx_ref.matmul(mx_ref.quantize(e.reshape(128, 512).astype(BF)), (c.reshape(128, 8), np.full((16, 2), 127, np.uint8))).T.reshape(-1).astype(np.float64)
CODE_VALUE, SCALE_VALUE = values_of_codes(), 2.0 ** (np.arange(256) - 127.0)
def decode(q):
    return (CODE_VALUE[q[0]].reshape(16, 8, -1, 4) * SCALE_VALUE[q[1]][:, None, :, None] + 0.0).reshape(128, -1).astype(np.float32)
def f(rng, *shape):
    return mx_ref.flush((rng.standard_normal(shape, dtype=np.float32) * np.exp2(rng.integers(-2, 3, shape[:-1] + (1,)))).astype(BF))
def wide(rng, *shape, cols=0):
    v = rng.standard_normal(shape, dtype=np.float32) * np.exp2(rng.integers(-12, 13, shape)).astype(np.float32)
    if cols: v *= np.repeat(np.exp2(rng.integers(-cols, cols + 1, shape[:-2] + (1, shape[-1] // 4))) * (rng.random(shape[:-2] + (1, shape[-1] // 4)) > 0.0625), 4, axis=-1).astype(np.float32)
    return mx_ref.flush(v.astype(BF))
C, A, B, E, F, R = 384, 160, 96, 64, 6, 3
STEP = [1, 2]
def order(p):
    return np.argsort(-(p[::16] + np.float32(0.0)), axis=1, kind="stable")
def gput(t, e, h):
    a, b = t.reshape(8, 16, -1, 4).copy(), h.reshape(8, 16, -1, 4)
    for g in range(8): a[g][:, e[g]] = b[g]
    return a.reshape(128, -1)
def big(v):
    v = v.astype(np.float32)
    v[np.abs(v) < np.float32(2.0 ** -16)] = 0
    return v.astype(BF)
def numbers_of(rng):
    return {"x": big(f(rng, N, 128, 4 * C)), "u": np.array(f(rng, N, 128, 512)), "v": np.array(f(rng, N, 128, 512))}
def layers(rng):
    return big(f(rng, N, 128, 2048)).reshape(N, 8, 16, 4, 8, 16, 4)
def apart(w, k):
    w[:, :, :k] = 0
    w[:, :, :, :, :, :k] = 0
    return w
def holding(w, k):
    w = apart(w, k).reshape(N, 128, 4, 128, 4)
    i = np.flatnonzero(np.arange(128) % 16 < k)
    for b in range(4): w[:, i, b, i, b] = 32
    return w
def weights(rng, w):
    c, p = packed(np.ascontiguousarray(w).reshape(N, 128, 2048), rng)
    return {"wc": c, "ws": p}
def signs(rng):
    return np.stack([rng.permutation(8) % 2 * 2.0 - 1.0 for r in range(N)])
def setup_inputs(rng):
    return {**numbers_of(rng), **weights(rng, layers(rng))}
def setup_inputs_ties(rng):
    d = numbers_of(rng)
    e = rng.permutation(N)
    x = d["x"].reshape(N, 8, 16, C, 4)
    for r in range(N):
        k = np.zeros(C, int) if r == e[0] else rng.permutation(C) % 3
        a = x[r][:, :8, :3].copy()
        a[:, :, 2] = 0
        x[r][:, :8] = a[:, :, k]
    x[e[1]] = 0
    u = d["u"].reshape(N, 8, 16, 128, 4)
    u[:, :, 8:, ::16] = 0
    return {"x": x.reshape(N, 128, 4 * C), "u": u.reshape(N, 128, 512), "v": d["v"], **weights(rng, holding(layers(rng), 8))}
def setup_inputs_near(rng):
    d = numbers_of(rng)
    x = np.zeros((N, 8, 16, C, 4), np.float32)
    u = d["u"].reshape(N, 128, 128, 4)
    u[:, :, ::16] = 0
    o, c = rng.permutation(N) % 4, signs(rng)
    upper = np.arange(C) // (C // 2)
    for r in range(N):
        i = (np.arange(C) + rng.integers(0, C, (8, 1))) % C
        if o[r] == 3: i = i % (C // 2) * 2 + upper
        s = (i + 1) // 2
        size = 1.0 if o[r] < 2 else 2.0 ** -4
        g = ((s[:, :, None] >> np.arange(8)) & 1) * np.exp2(np.arange(8) - 23.0) * size
        if o[r] < 2: x[r, :, 0, :, 0] = c[r][:, None]
        if o[r] == 3: x[r, :, 0, :, 0] = (8 + upper) * 2.0 ** -30
        x[r, :, 8] = g[:, :, :4]
        x[r, :, 9] = g[:, :, 4:]
        x[r, :, 10:] = rng.integers(4, 8, (8, 6, C, 4)) * 2.0 ** -20 * size
        k = 1.0 if o[r] == 0 else 2.0 ** -30
        for h in range(0, 128, 16):
            u[r, h, h, 0] = k
            u[r, h + 8:h + 10, h] = k
    w = (np.abs(layers(rng).astype(np.float32)) * np.float32(0.125)).astype(BF)
    return {"x": x.reshape(N, 128, 4 * C).astype(BF), "u": u.reshape(N, 128, 512), "v": d["v"], **weights(rng, holding(w, 10))}
def setup_inputs_huge(rng):
    d = numbers_of(rng)
    c = np.stack([rng.permutation(C) % 2 * 2.0 - 1.0 for r in range(N)])
    c[rng.permutation(N) < N // 2] = -1
    x = (0.6 + 0.2 * rng.random((N, 128, C, 4))) * np.where(c < 0, -2.0 ** 30, 2.0 ** 28)[:, None, :, None]
    u = d["u"].reshape(N, 128, 128, 4)
    a = 2.0 ** 30 * (1 - 0.25 * rng.random((N, 128, 8, 4))) * signs(rng)[:, None, :, None]
    u[:, :, ::16] = a.astype(np.float32).astype(BF)
    return {"x": x.astype(np.float32).reshape(N, 128, 4 * C).astype(BF), "u": u.reshape(N, 128, 512), "v": d["v"], **weights(rng, holding(layers(rng), 16))}
def setup_inputs_levels(rng):
    d = numbers_of(rng)
    x = d["x"].reshape(N, 8, 16, C, 4)
    x[:, :, :8] = 0
    x[:, :, 1, :, 0] = 1
    for r in range(N):
        n = rng.permutation(np.array([0, 1, B - 1, B, B + 1, C - A - B, C - A - max(B, A // 2), rng.integers(0, C - A - B + 1)]))
        way = rng.permutation(8)
        for g in range(8):
            k = rng.permutation(C)[:A]
            if way[g] == 0: k = np.arange(A)
            if way[g] == 1: k = np.arange(C - A, C)
            s = rng.integers(1, 8, C)
            s[k] = rng.integers(8, 16, A)
            rest = np.setdiff1d(np.arange(C), k)[B:]
            e = rng.permutation(rest)[:n[g]]
            s[e] = -s[e]
            x[r, g, 0, :, 0] = (s * 0.125).astype(np.float32).astype(BF)
    u = d["u"].reshape(N, 128, 128, 4)
    u[:, :, ::16] = 0
    for h in range(0, 128, 16): u[:, h, h, 0] = 1
    w = apart(layers(rng), 8)
    half = rng.permutation(N)[:N // 2]
    for g in range(8):
        w[:, g, 1, 0, g, 1, 0] = 64
        for r in half: w[r, g, 1, 0, g, 0, 0] = -0.5
    return {"x": x.reshape(N, 128, 4 * C), "u": u.reshape(N, 128, 512), "v": d["v"], **weights(rng, w)}
def setup_inputs_spread(rng):
    d = setup_inputs(rng)
    d["x"] = big(wide(rng, N, 128, 4 * C, cols=6))
    return d
def check_inputs(d):
    b = []
    for k in ("x", "u", "v"):
        a = np.abs(d[k].astype(np.float32))
        if not (np.isfinite(a).all() and ((a == 0) | (a >= 2.0 ** -30) & (a <= 2.0 ** 30)).all()): b.append("a value of " + k)
    none, least, most = [emit(mx_ref.quantize(np.full((128, 16), k, np.float32).astype(BF)))[1][0, 0] for k in (0.0, 2.0 ** -30, 2.0 ** 30)]
    for r in range(N):
        if ((d["wc"][r] == 0x7F) | (d["wc"][r] == 0xFF)).any(): b.append("wc: a code that is no number")
        s = mx_ref.live(d["ws"][r])
        if ((s != none) & ((s < least) | (s > most))).any(): b.append("ws: a scale out of range")
    return b
def reference(x, u, v, wc, ws):
    qu = [mx_ref.quantize(u[r]) for r in range(N)]
    lay = [pk(wc[r], ws[r]) for r in range(N)]
    kept = [np.concatenate([x[r], np.zeros((128, 4 * C * R), BF)], axis=1) for r in range(N)]
    level = np.zeros((N, 8, C), np.int64)
    border = [decode(mx_ref.quantize(np.ascontiguousarray(x[r - 1][:, 4 * (C - E):]))).astype(BF) for r in range(N)]
    for t in range(R):
        sent = []
        for r in range(N):
            had = level[r].copy()
            o = order(mx_ref.matmul(qu[r], mx_ref.quantize(gcols(kept[r], had * C + np.arange(C)))))
            going, others = o[:, :A], np.sort(o[:, A:], axis=1)
            low = np.argsort(np.take_along_axis(had, others, axis=1), axis=1, kind="stable")[:, :B]
            e = np.concatenate([going, np.take_along_axis(others, low, axis=1)], axis=1)
            l = np.take_along_axis(had, e, axis=1)
            q = (R + 1) * C + e // F
            for k in range(F - 1, 0, -1):
                found = (e % F >= k) & (np.take_along_axis(had, np.maximum(e - k, 0), axis=1) >= l)
                q = np.where(found, l * C + e - k, q)
            a = gcols(kept[r], l * C + e).astype(np.float32)
            b = gcols(np.concatenate([kept[r], border[r]], axis=1), q).astype(np.float32)
            z = mx_ref.quantize(((a + b) * np.float32(0.5)).astype(BF))
            h = tile([mx_ref.matmul(pick(lay[r], np.arange(128 * i, 128 * i + 128)), z) * np.float32(0.03125) for i in range(4)])
            kept[r] = gput(kept[r], (l + 1) * C + e, h)
            np.put_along_axis(level[r], e, l + 1, axis=1)
            sent.append(mx_ref.quantize(gcols(h, np.argsort(going, axis=1)[:, A - E:])))
        if t < R - 1: border = [decode(sent[r - STEP[t]]).astype(BF) for r in range(N)]
    y, ol = np.zeros((N, 128, C), np.float32), np.zeros((N, 8, C), np.float32)
    oc, osc = np.zeros((N, 128, 4 * C), np.uint8), np.zeros((N, 16, C), np.uint8)
    for r in range(N):
        q = mx_ref.quantize(gcols(kept[r], level[r] * C + np.arange(C)))
        y[r] = mx_ref.matmul(mx_ref.quantize(v[r]), q)
        ol[r] = level[r]
        oc[r], osc[r] = emit(q)
    return {"y": y, "ol": ol, "oc": oc, "osc": osc}

from concourse.mybir import dt, AluOpType, ActivationFunctionType

OP = AluOpType
AF = ActivationFunctionType
C, A, B, E, F, R = 384, 160, 96, 64, 6, 3
NZ = A + B
STEP = [1, 2]
HB = [384, 704, 1024]
BB = [None, 640, 960]
WCOLS = 1280
TW = [128, 128, 192, 256, 320, 384]
SROWS = [[11, 10, 23, 22, 19, 18, 15, 14, 13], [11, 10, 23, 19, 15, 14], [11, 10, 23, 19, 15, 14]]
PEORD = [5, 1, 0, 2, 4, 3]
SPLIT = 192
ZSDMA = [(0, 14), (14, 24)]
ZH = [18, 12]
EV = [[0, 1, 2, 3], [2, 3]]
XV = [2, 3]
BANK = [["pS0", "pS1", "pC", "pO"], ["pR0", "pR1", "pR2", "pR3"]]
NTMP = 10
NENG = 4
COST = dict(cyc=0.83 * 1.25, gath=1.56, scat=3.8, act=60.0, same=60.0, other=110.0, pe=0.63, dma=1700.0, bw=180.0, rx=3000.0)
SEARCH, STEPS, HEAT = 20, 30000, 600.0
BF, F32, F16, I32, U16, X4, U8 = "bfloat16", "float32", "float16", "int32", "uint16", "float8_e4m3fn_x4", "uint8"
BYTES = {BF: 2, F16: 2, U16: 2, F32: 4, I32: 4, X4: 4, U8: 1}

SCRATCH = {}
PART = {}


def _s(name, n, d, where="sbuf"):
    SCRATCH[name] = (where, [128, n], d)


def _pool(buf, d, parts):
    at = 0
    for name, n in parts:
        PART[name] = (buf, at, n)
        at += (n + 7) // 8 * 8
    _s(buf, at, d)


for _n, _w, _d in [
    ("xn", 4 * C, BF), ("W0", WCOLS, BF), ("W1", WCOLS, BF), ("W2", WCOLS, BF), ("W3", WCOLS, BF),
    ("X", 4 * C, BF), ("Z", 4 * NZ, BF), ("Tt", 512, BF), ("zs", 4 * C, BF),
    ("ut", 512, BF), ("vt", 512, BF), ("one", 512, BF), ("Eb", 2048, BF), ("Wb", 512, BF), ("Wc", 512, BF), ("Wo", 512, BF), ("cnt", 512, BF),
    ("uq", 128, X4), ("us", 128, U8), ("urq", 128, X4), ("urs", 128, U8), ("vq", 128, X4), ("vs", 128, U8),
    ("wq", 512, X4), ("wsc", 512, U8), ("Eq", 512, X4), ("Es", 512, U8), ("Wcq", 128, X4), ("Wcs", 128, U8),
    ("Woq", 128, X4), ("Wos", 128, U8), ("cnq", 128, X4), ("cns", 128, U8),
    ("xnq", C, X4), ("xns", C, U8), ("x0q", C, X4), ("x0s", C, U8), ("xq", C, X4), ("xs", C, U8),
    ("fq", C, X4), ("fs", C, U8), ("zq", NZ, X4), ("zsc", NZ, U8),
    ("t0q", 128, X4), ("t0s", 128, U8), ("t1q", 128, X4), ("t1s", 128, U8), ("lq", 256, X4), ("ls", 256, U8),
    ("i16", C, BF), ("ph4", C, F32), ("lg4", C, F32), ("dm", C, BF), ("rst", C, BF), ("mixm", 2 * C, BF), ("rs4", NZ, BF),
    ("msk", C, F32), ("own", C, F32), ("mi", 2 * C, F32), ("mix", 2 * C, F32), ("J", 24 * 192, BF),
    ("cm", C, F16), ("dsc", C, F16), ("L", C, F32), ("Lm", NZ, F16), ("Ls", NZ, F16), ("cR", C, F32), ("junk", 2 * C, BF), ("yb", C, F32), ("lev", 32, F32),
]:
    _s(_n, _w, _d)
_pool("ki", I32, [("pi", 2), ("ti", 24), ("uof", 8)])
_pool("kf", F32, [("col", 8), ("c24", 24), ("mq", 4), ("logi", 24), ("lg1", 24), ("rsc", 216), ("thk", 48), ("bst", 72), ("r0", 72), ("ones", 72), ("tb4", 4), ("ka", 24), ("kb", 24)])
_pool("ku", U16, [("uo", 8), ("offx", 24), ("offn", 24)])
_pool("df", F32, [("rsS", 24), ("base", 24), ("bt", 72), ("thr", 72), ("rank", 24), ("fl", 72), ("sc", 72), ("sc2", 72), ("pen", 72), ("cand", 96), ("cso", 96),
                  ("sel", 24), ("new", 24), ("top", 24), ("A1", 26), ("A2", 26), ("kp", 48), ("nk", 48), ("ap", 48), ("rsn", 48), ("ra", 24), ("rt", 72),
                  ("ng", 24), ("ta", 24), ("acA", 4), ("acB", 4), ("tA", 16), ("tB", 16), ("sg", 24)])
_pool("du", U16, [("po", 24), ("zo", 64), ("xo", 24), ("ro", 24), ("co", 24), ("tof", 16)])
for _i in range(6):
    _s("ct%d" % _i, 4 * TW[_i], BF)
    _s("cq%d" % _i, TW[_i], X4)
    _s("cs%d" % _i, TW[_i], U8)
for _i in range(NTMP):
    _s("sg%d" % _i, C, BF)
for _n in ("pS0", "pS1", "pC", "pO", "pR0", "pR1", "pR2", "pR3"):
    _s(_n, 512, F32, "psum")
SEMAPHORES = ["cv", "cs", "ct", "cg", "arr0", "arr1", "arr2", "snt"] + ["d%d" % _i for _i in range(28)]


def v(name, a=0, b=None, st=1):
    if name in PART:
        buf, at, n = PART[name]
        return (buf, at + a, at + (n if b is None else b), st)
    return (name, a, SCRATCH[name][1][1] if b is None else b, st)


def cols(x):
    return len(range(x[1], x[2], x[3]))


def ind(win, off):
    return ("@", win, off)


def isview(x):
    return isinstance(x, tuple)


def ap(T, x, cast=None):
    if not isview(x):
        return x
    if x[0] == "@":
        return ap(T, x[1], cast).indirect(ap(T, x[2]))
    a = T[x[0]][:, x[1]:x[2]] if x[3] == 1 else T[x[0]][:, x[1]:x[2]:x[3]]
    return a.bitcast(cast) if cast is not None else a


def flat(xs):
    out = []
    for x in xs:
        if isview(x):
            out += [x[1], x[2]] if x[0] == "@" else [x]
    return out


def build():
    ops = []
    CYC, GATH, SCAT = COST["cyc"], COST["gath"], COST["scat"]

    def op(eng, fn, rd, wr, cost, kind="c", lat=0.0, after=(), acc=False):
        ops.append(dict(eng=eng, fn=fn, rd=flat(rd), wr=flat(wr), cost=cost, kind=kind, lat=lat, after=list(after), acc=acc, soft=[]))
        return len(ops) - 1

    def n_of(x):
        return 16 * cols(x[2]) if x[0] == "@" else cols(x)

    def two(*xs):
        return all(BYTES[SCRATCH[x[0]][2]] == 2 for x in xs)

    def vc(n, rate):
        return max(64, n * rate) * CYC

    def sb(x):
        return SCRATCH[x[0]][0] == "sbuf"

    def tt(o, a, b, f):
        c = 50 + n_of(a) * GATH * CYC if a[0] == "@" else vc(cols(o), 2 if sb(a) and sb(b) else 1)
        return op("v", lambda q, T: q.tensor_tensor(ap(T, o), ap(T, a), ap(T, b), f), [a, b], [o], c)

    def ts(o, a, s1, f0, s2=None, f1=None):
        c = 50 + n_of(a) * GATH * CYC if a[0] == "@" else vc(cols(o), 0.5 if two(o, a) else 1)
        if f1 is None:
            return op("v", lambda q, T: q.tensor_scalar(ap(T, o), ap(T, a), ap(T, s1), None, f0), [a, s1], [o], c)
        return op("v", lambda q, T: q.tensor_scalar(ap(T, o), ap(T, a), ap(T, s1), ap(T, s2), f0, f1), [a, s1, s2], [o], c)

    def cp(o, a, cast=None):
        if o[0] == "@":
            return op("v", lambda q, T: q.tensor_copy(ap(T, o), ap(T, a)), [a, o[2]], [o[1]], 50 + cols(a) * SCAT * CYC)
        c = 50 + n_of(a) * GATH * CYC if a[0] == "@" else vc(cols(o), 0.5 if two(o, a) else 1)
        return op("v", lambda q, T: q.tensor_copy(ap(T, o, cast), ap(T, a, cast)), [a], [o], c)

    def ms(o, val):
        return op("v", lambda q, T: q.memset(ap(T, o), val), [], [o], vc(cols(o), 0.5 if two(o) else 1))

    def scan(o, d0, d1, f0, f1, init=0.0):
        return op("v", lambda q, T: q.tensor_tensor_scan(ap(T, o), ap(T, d0), ap(T, d1), init, f0, f1), [d0, d1], [o], vc(cols(o), 0.5 if two(o, d0, d1) else 1))

    def act(o, a, f, bias=None, scale=None, accum=None):
        c = 65 + n_of(a) * GATH * CYC if a[0] == "@" else COST["act"] + cols(o) * CYC + (20 if accum else 0)

        def fn(q, T):
            kw = {}
            if bias is not None:
                kw["bias"] = ap(T, bias)
            if scale is not None:
                kw["scale"] = ap(T, scale)
            if accum is not None:
                kw["accum_out"] = ap(T, accum)
            return q.activation(ap(T, o), ap(T, a), f, **kw)
        return op("s", fn, [a, bias, scale], [o, accum], c)

    def quant(oc, osx, a):
        return op("v", lambda q, T: q.quantize_mx(ap(T, oc), ap(T, osx), ap(T, a)), [a], [oc, osx], (12 + 0.22 * cols(a)) * CYC / 0.83)

    def mm(o, lc, ls, rc, rs, start=True, stop=True):
        return op("t", lambda q, T: q.matmul_mx(ap(T, o), ap(T, lc), ap(T, ls), ap(T, rc), ap(T, rs), start, stop),
                  [lc, ls, rc, rs], [o], (cols(o) + 16) * COST["pe"], lat=60.0, acc=not start)

    def iota(o, pat, base=0, ch=0):
        fl = SCRATCH[o[0]][2] != I32
        return op("g", lambda q, T: q.iota(ap(T, o), pat, base, ch, allow_small_or_imprecise_dtypes=True) if fl else q.iota(ap(T, o), pat, base, ch),
                  [], [o], 130 + 2 * cols(o) * CYC)

    def sel(o, a, pat, f, base, ch):
        return op("g", lambda q, T: q.affine_select(ap(T, o), ap(T, a), pat, f, 0.0, base, ch), [a], [o], 170 + 2 * cols(o) * CYC)

    def dma(eng, fn, rd, wr, nbytes, after=()):
        return op(eng, fn, rd, wr, 100.0 if eng != "g" else 700.0, kind="d", lat=COST["dma"] + nbytes / COST["bw"], after=after)

    def send(t, qc, qs, step):
        a = op("g", (t, qc, qs, step), [qc, qs], [], 1200.0, kind="send")
        op("rx", t, [], [v("lq", 64 + 64 * t, 128 + 64 * t), v("ls", 64 + 64 * t, 128 + 64 * t)], 0.0, kind="rx", lat=COST["rx"] + (0.0 if t else 1500.0), after=[a])

    col = lambda j: v("col", j, j + 1)
    seg = lambda name, l: v(name, 24 * l, 24 * l + 24)
    R16, R4, RQ, R24, R4X = range(5)

    lx0 = dma("y", lambda q, T: q.dma_start(T.xn[:, 0:768], T.x[:, 0:768]), [], [v("xn", 0, 768)], 200000)
    lx1 = dma("s", lambda q, T: q.dma_start(T.xn[:, 768:1536], T.x[:, 768:1536]), [], [v("xn", 768, 1536)], 393000)
    lu = dma("y", lambda q, T: q.dma_start(T.ut[:], T.u[:]), [], [v("ut")], 524000)
    ops[lu]["soft"] = [lx0]
    first = [lx0, lx1, lu]
    iota(v("uof"), [[16, 8]])
    iota(v("pi", 0, 1), [[0, 1]], 0, 1)
    iota(v("c24"), [[1, 24]])
    iota(v("i16"), [[0, 24], [1, 16]])
    iota(v("ph4"), [[4, C]])
    iota(v("lg4"), [[4, 24], [96, 16]])
    iota(v("rs4"), [[0, NZ // 4], [4096, 4]])
    RSC = [0, 48, 120]
    for t in range(R):
        iota(v("rsc", RSC[t], RSC[t] + 24 * (t + 2)), [[0, 24], [8192, t + 2]], -4096)
    iota(v("ones"), [[0, 72]], 1)
    ms(v("one"), 1.0)
    sel(v("Wb"), v("one"), [[-16, 8], [0, 64]], OP.is_ge, 0, 1)
    sel(v("Wc"), v("Wb"), [[16, 8], [0, 64]], OP.is_ge, 15, -1)
    for h in range(4):
        sel(v("Wo", h, 512, 4), v("Wc", h, 512, 4), [[1 if h < 2 else -1, 128]], OP.is_gt, 0, -1 if h < 2 else 1)
    for b in range(4):
        sel(v("Eb", 512 * b, 512 * b + 512), v("one"), [[-1, 512]], OP.is_equal, b, 4)
    cp(v("uo"), v("uof"))
    ts(v("pi", 1, 2), v("pi", 0, 1), 15, OP.bitwise_and)
    ts(v("ti", 0, 1), v("pi", 0, 1), 3, OP.bitwise_and)
    cp(col(R16), v("pi", 1, 2))
    cp(col(R4), v("ti", 0, 1))
    ts(col(R24), v("pi", 1, 2), 24.0, OP.mult)
    ts(col(R4X), v("pi", 1, 2), 4.0, OP.mult)
    tt(col(RQ), col(R16), col(R4), OP.subtract)
    ts(v("logi"), v("c24"), col(R24), OP.add)
    ts(v("lg1"), v("logi"), 1.0, OP.add)
    cp(v("offx"), v("logi"))
    ts(v("dm"), v("i16"), col(R16), OP.is_equal)
    ts(v("rst"), v("i16"), 0.0, OP.not_equal)
    ms(v("mixm", 0, 2 * C, 2), 0.0)
    ts(v("mixm", 1, 2 * C, 2), v("i16"), col(R16), OP.is_le)
    ts(v("mq"), v("c24", 0, 4), 4.0, OP.mult, col(RQ), OP.is_equal)
    ts(v("tb4"), v("c24", 0, 4), -64.0, OP.mult, col(R4X), OP.subtract)
    ts(v("tb4"), v("tb4"), -float(4 * (A - E) + 2), OP.add)
    for l in (1, 2):
        ms(seg("thk", l - 1), float(l))
    ms(v("thk", 0, 48, F), -1.0)
    ms(v("bst"), 0.0)
    ts(v("ka"), v("logi"), -1.0, OP.add)
    for t in (1, 2):
        ts(v("bst", 24 * t, 24 * t + 24, F), v("c24", 0, 4), col(R4X), OP.add, float(BB[t]), OP.add)
        tt(seg("r0", t), v("ka"), seg("bst", t), OP.max)
    for i in range(1, 6):
        ms(v("ct%d" % i, 4 * TW[i] - 256, 4 * TW[i]), 0.0)
    ms(v("ct0"), 0.0)
    iota(v("J", 191, 24 * 192, 192), [[-16, 24]], C - A)
    ms(v("rsS"), 0.0)
    ms(v("cnt"), 0.0)
    ms(v("Tt", 256, 512), 0.0)
    ms(v("lev"), 0.0)
    ms(v("A1"), 0.0)
    ms(v("A2"), 0.0)
    cp(v("top"), v("logi"))
    quant(v("Wcq"), v("Wcs"), v("Wc"))
    quant(v("Eq"), v("Es"), v("Eb"))
    quant(v("Woq"), v("Wos"), v("Wo"))
    ts(v("kb"), v("c24"), 16.0, OP.mult, col(R16), OP.add)
    ts(v("ti"), v("kb"), -11.5, OP.add, 1.0 / 24.0, OP.mult)
    ts(v("ka"), v("ti"), -383.0 / 16.0, OP.mult)
    tt(v("ka"), v("ka"), v("kb"), OP.add)
    ts(v("offn"), v("ka"), 16.0, OP.mult)
    quant(v("uq"), v("us"), v("ut"))
    cp(v("urq"), ind(v("uq"), v("uo")), dt.uint32)
    act(v("urs"), ind(v("us"), v("uo")), AF.Copy)
    quant(v("xnq", 0, 192), v("xns", 0, 192), v("xn", 0, 768))
    quant(v("xnq", 192, C), v("xns", 192, C), v("xn", 768, 4 * C))
    cp(v("x0q"), ind(v("xnq"), v("offx")), dt.uint32)
    act(v("x0s"), ind(v("xns"), v("offx")), AF.Copy)
    send(0, v("xnq", C - E, C), v("xns", C - E, C), 1)
    dma("y", lambda q, T: q.dma_start(T.lq[:, 0:64].bitcast(dt.uint8), T.xnq[:, 0:64].bitcast(dt.uint8)), [v("xnq", 0, 64)], [v("lq", 0, 64)], 32768)
    dma("y", lambda q, T: q.dma_start(T.ls[:, 0:64], T.xns[:, 0:64]), [v("xns", 0, 64)], [v("ls", 0, 64)], 8192)
    dma("y", lambda q, T: q.dma_start(T.zs[:], T.x[:]), [], [v("zs")], 393216, after=first)
    dma("g", lambda q, T: q.dma_start(T.zs[:, 4:4 * C], T.x[:, 0:4 * C - 4], accum_op=OP.add), [v("zs")], [v("zs")], 800000)
    dma("y", lambda q, T: q.dma_start(T.wq[:].bitcast(dt.uint8), T.wc[:]), [], [v("wq")], 500000, after=first)
    dma("y", lambda q, T: q.dma_start(T.wsc[:], T.ws[:]), [], [v("wsc")], 500000, after=first)
    dma("y", lambda q, T: q.dma_start(T.vt[:], T.v[:]), [], [v("vt")], 600000, after=first)
    quant(v("vq"), v("vs"), v("vt"))
    for b in range(4):
        sel(v("W%d" % b, 0, C), v("xn", b, 4 * C, 4), [[0, C]], OP.is_ge, 0, 0)

    def unpack(t):
        for b in range(4):
            mm(v("pR%d" % b, 0, 128), v("Eq", 128 * b, 128 * b + 128), v("Es", 128 * b, 128 * b + 128), v("lq", 64 * t, 64 * t + 128), v("ls", 64 * t, 64 * t + 128))
            if t == 0:
                tt(v("zs", b, 4 * C, 4 * F), v("pR%d" % b, 64, 128), v("xn", b, 4 * C, 4 * F), OP.add)
            else:
                act(v("W%d" % b, BB[t], BB[t] + E), v("pR%d" % b, 64, 128), AF.Copy)

    def adding(a, z):
        return lambda q, T: q.dma_start(T.zs[:, 64 * a:64 * z], T.X[:, 64 * a:64 * z], accum_op=OP.add)

    lev, levs = v("lev", 1, 25), v("lev", 0, 24)
    tg = []
    for t in range(R):
        nl = t + 1
        xq, xs = ("x0q", "x0s") if t == 0 else ("xq", "xs")
        mm(v("pS0", 0, C), v("urq"), v("urs"), v(xq), v(xs))
        mm(v("pS1", 0, C), v("urq"), v("urs"), v(xq), v(xs))
        ops[tt(v("msk"), v("pS0", 0, C), v("dm"), OP.mult)]["after"] += [j for j in tg if ops[j]["eng"] == "v"]
        for a, b in ((0, SPLIT), (SPLIT, C)):
            scan(v("own", a, b), v("rst", a, b), v("msk", a, b), OP.mult, OP.add)
            ops[act(v("mi", 2 * a, 2 * b, 2), v("pS1", a, b), AF.Abs, bias=2.0 ** -122, scale=0.625 * 2.0 ** -23)]["after"] += [j for j in tg if ops[j]["eng"] == "s"]
            act(v("mi", 2 * a + 1, 2 * b, 2), v("pS1", a, b), AF.Copy)
            scan(v("mix", 2 * a, 2 * b), v("mixm", 2 * a, 2 * b), v("mi", 2 * a, 2 * b), OP.mult, OP.add)
        if t:
            for l in range(nl):
                act(seg("thr", l), lev, AF.Abs, scale=8192.0, bias=-8192.0 * l)
        unpack(t)
        if t:
            for l in range(1, nl):
                tt(seg("kp", l - 1), levs, seg("thk", l - 1), OP.is_lt)
                tt(seg("ap", l - 1), v("A%d" % l, 0, 24), seg("bst", t), OP.max)
            w = 24 * t
            act(v("nk", 0, w), v("kp", 0, w), AF.Identity, scale=-1.0, bias=1.0)
            tt(v("ap", 0, w), v("ap", 0, w), v("nk", 0, w), OP.mult)
            scan(v("rsn", 0, w), v("kp", 0, w), v("ap", 0, w), OP.mult, OP.add)
            tt(seg("rt", 0), seg("r0", t), seg("thr", 0), OP.subtract)
            tt(v("rt", 24, 24 + w), v("rsn", 0, w), v("thr", 24, 24 + w), OP.subtract)
            tt(v("ra"), seg("rt", 0), seg("rt", 1), OP.max)
            if t == 2:
                tt(v("ra"), v("ra"), seg("rt", 2), OP.max)
            cp(v("ro"), v("ra"))
            if not ZSDMA:
                for b in range(4):
                    tt(v("zs", b, 4 * C, 4), ind(v("W%d" % b, 0, HB[t]), v("ro")), v("X", b, 4 * C, 4), OP.add)
            for a, z in ZSDMA or ():
                for b in range(4):
                    act(v("zs", 64 * a + b, 64 * z, 4), ind(v("W%d" % b, 0, HB[t]), v("ro", a, z)), AF.Copy)
                dma("g", adding(a, z), [v("zs", 64 * a, 64 * z), v("X", 64 * a, 64 * z)], [v("zs", 64 * a, 64 * z)], 25000 * (z - a))
        for i in PEORD:
            ct = "ct%d" % i
            for k in range(4 * i + 3, 4 * i - 1, -1):
                s, w, o = k % 4, 16 * k, v("own", 16 * k + 15, 16 * k + 16)
                if k in SROWS[t]:
                    sg = "sg%d" % SROWS[t].index(k)
                    act(v(sg, 0, w), v("mix", 1, 2 * w, 2), AF.Sign, bias=o, scale=-1.0)
                    act(v(ct, s, 4 * w, 4), v(sg, 0, w), AF.Relu, scale=-1.0, accum=v("rsS", k, k + 1))
                    ts(v(ct, 4 * w + s, 4 * w + 64, 4), v("mix", 2 * w + 1, 2 * w + 32, 2), o, OP.is_gt)
                else:
                    ts(v(ct, s, 4 * w + 64, 4), v("mix", 1, 2 * w + 32, 2), o, OP.is_gt)
                    if k:
                        scan(v("J", 192 * k + 192 - w // 2, 192 * k + 192), v(ct, s, 2 * w, 4), v(ct, 2 * w + s, 4 * w, 4), OP.add, OP.add, float(C - A - w))
            quant(v("cq%d" % i), v("cs%d" % i), v(ct))
            mm(v("pC", 0, TW[i]), v("Wcq"), v("Wcs"), v("cq%d" % i), v("cs%d" % i), i == PEORD[0], i == PEORD[-1])
        w = 24 * nl
        tt(v("base"), v("J", 191, 24 * 192, 192), v("rsS"), OP.add)
        if t + 1 < R and set(SROWS[t]) != set(SROWS[t + 1]):
            iota(v("J", 191, 24 * 192, 192), [[-16, 24]], C - A)
            iota(v("rsS"), [[0, 24]])
        if t:
            for l in range(nl):
                tt(seg("bt", l), v("base"), seg("thr", l), OP.subtract)
        ahead = ("zs", "vq", "ku") if t and not ZSDMA else ("Eq", "Woq")
        ops[tt(v("cm"), v("pC", 0, C), v("dm"), OP.mult)]["after"] += [j for j in range(len(ops) - 1) if ops[j]["eng"] in "vs" and ops[j]["kind"] == "c" and ops[j]["wr"][0][0] in ahead]
        scan(v("dsc"), v("rst"), v("cm"), OP.mult, OP.add)
        d = v("dsc", 15, C, 16)
        for l in range(nl):
            tt(seg("fl", l), seg("bt", l) if t else v("base"), d, OP.is_ge)
        scan(v("sc", 0, w), v("ones", 0, w), v("fl", 0, w), OP.mult, OP.add)
        ends = v("sc", 23, w, 24)
        ts(v("cnt", 0, 4 * nl, 4), ends, 12.0, OP.min)
        act(v("cnt", 1, 4 * nl, 4), ends, AF.Relu, bias=-12.0)
        if t:
            low = v("sc", 23, w - 24, 24)
            ts(v("cnt", 6, 4 * nl, 4), low, 12.0, OP.min)
            ts(v("cnt", 7, 4 * nl, 4), low, -12.0, OP.add, 0.0, OP.max)
        if t == 1:
            ts(v("cnt", 12, 13), v("sc", 47, 48), 12.0, OP.min)
            act(v("cnt", 13, 14), v("sc", 47, 48), AF.Relu, bias=-12.0)
        quant(v("cnq"), v("cns"), v("cnt"))
        mm(v("pO", 0, 128), v("Woq"), v("Wos"), v("cnq"), v("cns"))
        tt(v("rank"), v("base"), d, OP.subtract)
        m = nl + 1
        ts(v("cand", 0, 24 * m, m), v("rank"), float(A), OP.add, float(A - 1), OP.min)
        act(v("pen", 0, w), v("fl", 0, w), AF.Identity, scale=2048.0, bias=float(A - 1 - 2048))
        tt(v("sc2", 0, w), v("sc", 0, w), v("pen", 0, w), OP.add)
        for l in range(nl):
            ts(v("cand", l + 1, 24 * m, m), seg("sc2", l), v("pO", l, l + 1), OP.add)
        scan(v("cso", 0, 24 * m), v("rsc", RSC[t], RSC[t] + 24 * m), v("cand", 0, 24 * m), OP.min, OP.max)
        pos = v("cso", m - 1, 24 * m, m)
        cp(v("po"), pos)
        co = []
        if t < R - 1:
            if t == 0:
                tt(v("ng"), v("lg1"), seg("sc", 0), OP.subtract)
            else:
                scan(v("ng"), seg("fl", 0), seg("fl", 1), OP.add, OP.add)
                tt(v("ng"), v("lg1"), v("ng"), OP.subtract)
            co = [ts(v("co"), v("ng"), v("pO", 3 * t, 3 * t + 1), OP.subtract)]
        ops[cp(ind(v("L"), v("po")), v("lg4" if t == 0 else "ph4"))]["after"] += co
        for c in range(4):
            ts(v("Lm", c, NZ, 4), v("L", c, NZ, 4), v("mq", c, c + 1), OP.mult)
        scan(v("Ls"), v("rs4"), v("Lm"), OP.min, OP.max)
        ts(v("zo"), v("Ls", 3, NZ, 4), col(R4), OP.add)
        for h in range(2):
            a, z = 32 * h, 32 * h + ZH[h]
            ts(v("Z", 16 * a, 16 * z), ind(v("zs"), v("zo", a, z)), 0.5, OP.mult)
            act(v("Z", 16 * z, 16 * a + 512), ind(v("zs"), v("zo", z, a + 32)), AF.Copy, scale=0.5)
            quant(v("zq", 128 * h, 128 * h + 128), v("zsc", 128 * h, 128 * h + 128), v("Z", 512 * h, 512 * h + 512))
        act(v("sg"), pos, AF.Sign, scale=-1.0, bias=NZ - 0.5)
        act(v("sel"), v("sg"), AF.Relu)
        act(v("new"), pos, AF.Identity, bias=float(HB[t]))
        tt(v("new"), v("new"), v("sg"), OP.mult)
        tt(v("top"), v("top"), v("new"), OP.max)
        cp(v("xo"), v("top"))
        if t == 0:
            act(v("A1", 1, 25), v("new"), AF.Copy)
        if t == 1:
            act(v("A2", 1, 25), v("new"), AF.Copy)
            tt(v("ta"), v("new"), seg("thr", 0), OP.subtract)
            tt(v("A1", 1, 25), v("A1", 1, 25), v("ta"), OP.max)
        tt(lev, lev, v("sel"), OP.add)
        if t == R - 1:
            dma("y", lambda q, T: q.dma_start(T.ol[:], T.lev[:, 1:25]), [lev], [], 12288)
        for h in range(2):
            for b in (0, 2, 1, 3):
                bank = v(BANK[h][b], 0, 128)
                mm(bank, v("wq", 128 * b, 128 * b + 128), v("wsc", 128 * b, 128 * b + 128), v("zq", 128 * h, 128 * h + 128), v("zsc", 128 * h, 128 * h + 128))
                o = v("W%d" % b, HB[t] + 128 * h, HB[t] + 128 * h + 128)
                if b in EV[h]:
                    ts(o, bank, 0.03125, OP.mult)
                else:
                    act(o, bank, AF.Copy, scale=0.03125)
        for b in range(4):
            win = ind(v("W%d" % b, 0, HB[t] + NZ), v("xo"))
            if b in XV:
                cp(v("X", b, 4 * C, 4), win)
            else:
                act(v("X", b, 4 * C, 4), win, AF.Copy)
        quant(v("xq"), v("xs"), v("X"))
        if t < R - 1:
            act(v("cR"), ind(v("ph4"), v("co")), AF.Copy)
            for c in range(4):
                j = (c % 2) * C
                act(v("junk", j, j + C - 16), v("cR", 0, C - 16), AF.Sign, bias=v("tb4", c, c + 1), accum=v("acA", c, c + 1))
                act(v("junk", j + C - 16, j + C), v("cR", C - 16, C), AF.Sign, bias=v("tb4", c, c + 1), accum=v("acB", c, c + 1))
            for b in range(4):
                act(v("tA", 4 * b, 4 * b + 4), v("acA"), AF.Identity, bias=32.0 + b, scale=-32.0)
                act(v("tB", 4 * b, 4 * b + 4), v("acB"), AF.Copy, scale=734.0)
            tt(v("tA"), v("tA"), v("tB"), OP.add)
            cp(v("tof"), v("tA"))
            for b in range(4):
                tg.append(act(v("Tt", b, 4 * E, 4), ind(v("X"), v("tof", 4 * b, 4 * b + 4)), AF.Copy))
            tg.append(quant(v("t%dq" % t), v("t%ds" % t), v("Tt")))
            send(t + 1, v("t%dq" % t, 0, E), v("t%ds" % t, 0, E), STEP[t])
    cp(v("fq"), ind(v("xq"), v("offn")), dt.uint32)
    act(v("fs"), ind(v("xs"), v("offn")), AF.Copy)
    H2 = C // 2
    mm(v("pS0", 0, H2), v("vq"), v("vs"), v("fq", 0, H2), v("fs", 0, H2))
    mm(v("pS1", 0, H2), v("vq"), v("vs"), v("fq", H2, C), v("fs", H2, C))
    dma("y", lambda q, T: q.dma_start(T.oc[:], T.fq[:].bitcast(dt.uint8)), [v("fq")], [], 196608)
    for j in range(4):
        dma("y", (lambda j: lambda q, T: q.dma_start(T.osc[4 * j:4 * j + 4, :], T.fs[32 * j:32 * j + 4, :]))(j), [v("fs")], [], 1536)
    act(v("yb", 0, H2), v("pS0", 0, H2), AF.Copy)
    cp(v("yb", H2, C), v("pS1", 0, H2))
    dma("s", lambda q, T: q.dma_start(T.y[:, 0:H2], T.yb[:, 0:H2]), [v("yb", 0, H2)], [], 150000)
    dma("y", lambda q, T: q.dma_start(T.y[:, H2:C], T.yb[:, H2:C]), [v("yb", H2, C)], [], 150000)
    return ops


def depend(ops):
    lastw, readers, bank = {}, {}, {}
    for i, o in enumerate(ops):
        dep = set(o["after"])
        for x in o["rd"] + o["wr"]:
            if SCRATCH[x[0]][0] == "psum":
                for j in bank.get(x[0], []):
                    if ops[j]["eng"] != o["eng"] or o["eng"] == "t":
                        dep.add(j)
        for x in o["rd"]:
            lw = lastw.setdefault(x[0], {})
            dep.update(lw[c] for c in range(x[1], x[2], x[3]) if c in lw)
        for x in o["wr"]:
            lw, rd = lastw.setdefault(x[0], {}), readers.setdefault(x[0], {})
            for c in range(x[1], x[2], x[3]):
                if c in lw:
                    dep.add(lw[c])
                dep.update(rd.get(c, ()))
        for x in o["rd"]:
            rd = readers.setdefault(x[0], {})
            for c in range(x[1], x[2], x[3]):
                rd.setdefault(c, []).append(i)
        for x in o["wr"]:
            lw, rd = lastw[x[0]], readers[x[0]]
            for c in range(x[1], x[2], x[3]):
                lw[c] = i
                rd.pop(c, None)
        for x in o["rd"] + o["wr"]:
            if SCRATCH[x[0]][0] == "psum":
                if o["eng"] == "t":
                    bank[x[0]] = [i]
                else:
                    bank.setdefault(x[0], []).append(i)
        dep.discard(i)
        o["dep"] = sorted(dep)


def place(ops, seq, pred, back):
    start, busy = {}, {}
    for i in seq:
        o = ops[i]
        t = 0.0
        for j, h in pred[i]:
            t = max(t, start[j] + ops[j]["cost"] + (o["lat"] if back else ops[j]["lat"]) + h)
        if back:
            t = max(t, o["lat"])
        row = busy.setdefault(o["eng"], [])
        n = len(row)
        k = 0
        while k < n and row[k][1] <= t:
            k += 1
        while k < n and row[k][0] < t + o["cost"]:
            t = max(t, row[k][1])
            k += 1
        row.insert(k, (t, t + o["cost"]))
        start[i] = t
    return start


def schedule(ops):
    n = len(ops)

    def hop(a, b):
        if ops[a]["eng"] == "t" and ops[b]["eng"] == "t":
            return 0.0
        return COST["same"] if ops[a]["eng"] == ops[b]["eng"] and ops[a]["kind"] == "c" else COST["other"]
    pred = [[(j, hop(j, i)) for j in ops[i]["dep"]] + [(j, -ops[j]["lat"]) for j in ops[i]["soft"]] for i in range(n)]
    succ = [[] for _ in range(n)]
    for i in range(n):
        for j, h in pred[i]:
            succ[j].append((i, h))
    tail = [0.0] * n
    for i in range(n - 1, -1, -1):
        tail[i] = ops[i]["cost"] + ops[i]["lat"] + max([h + tail[u] for u, h in succ[i]] + [0.0])

    def improve(seq, passes):
        top = None
        for _ in range(passes):
            fw = place(ops, seq, pred, False)
            total = max(fw[i] + ops[i]["cost"] + ops[i]["lat"] for i in range(n))
            if top is None or total < top[0]:
                top = (total, fw)
            bw = place(ops, sorted(range(n), key=lambda i: (-(fw[i] + ops[i]["cost"] + 1e-6 * i))), succ, True)
            seq = sorted(range(n), key=lambda i: (-(bw[i] + ops[i]["cost"]), i))
        return top
    best = improve(sorted(range(n), key=lambda i: (-tail[i], i)), 4)
    seed = [12345]

    def rnd():
        seed[0] = (seed[0] * 1103515245 + 12345) % 2147483648
        return seed[0] / 2147483648.0
    for it in range(SEARCH):
        key = dict(best[1])
        for _ in range(3):
            a = int(rnd() * n)
            key[a] -= 6000.0 * rnd() ** 2
        for i in range(n - 1, -1, -1):
            for j, h in pred[i]:
                key[j] = min(key[j], key[i] - 1e-3)
        got = improve(sorted(range(n), key=lambda i: (key[i], i)), 2)
        if got[0] <= best[0] + 30.0 * rnd():
            best = got
    fw = best[1]
    rows = {}
    for i in sorted(range(n), key=lambda i: (fw[i], i)):
        rows.setdefault(ops[i]["eng"], []).append(i)
    cost = [o["cost"] for o in ops]
    out = [[(u, ops[i]["cost"] + ops[i]["lat"] + h) for u, h in succ[i]] for i in range(n)]
    end = [o["cost"] + o["lat"] for o in ops]
    deg = [len(p) for p in pred]

    def run():
        nxt, left = [-1] * n, deg[:]
        for row in rows.values():
            for a, b in zip(row, row[1:]):
                nxt[a] = b
                left[b] += 1
        at, why = [0.0] * n, [-1] * n
        todo = [i for i in range(n) if not left[i]]
        for i in todo:
            s = at[i]
            for u, d in out[i]:
                if s + d > at[u]:
                    at[u] = s + d
                    why[u] = i
                left[u] -= 1
                if not left[u]:
                    todo.append(u)
            u = nxt[i]
            if u >= 0:
                if s + cost[i] > at[u]:
                    at[u] = s + cost[i]
                    why[u] = -2 - i
                left[u] -= 1
                if not left[u]:
                    todo.append(u)
        if len(todo) < n:
            return None
        last = max(range(n), key=lambda i: at[i] + end[i])
        held, i = [], last
        while why[i] != -1:
            if why[i] < -1:
                held.append(i)
                i = -2 - why[i]
            else:
                i = why[i]
        return at[last] + end[last], at, held, todo
    cur = run()
    top = cur
    for it in range(STEPS):
        if not cur[2]:
            break
        b = cur[2][int(rnd() * len(cur[2]))]
        row = rows[ops[b]["eng"]]
        p = row.index(b)
        far = 1 + int(rnd() ** 3 * 40)
        if rnd() < 0.5:
            a, z = p, max(0, p - far)
        else:
            a, z = p - 1, min(len(row) - 1, p - 1 + far)
        row.insert(z, row.pop(a))
        got = run()
        if got is not None and got[0] <= cur[0] + HEAT * (1.0 - it / STEPS) * rnd() ** 2:
            cur = got
            if got[0] < top[0]:
                top = got
        else:
            row.insert(a, row.pop(z))
    for i in range(n):
        ops[i]["t0"] = top[1][i]
    return top[3], top[0]


PLAN = {}


def plan():
    if not PLAN:
        ops = build()
        depend(ops)
        order, total = schedule(ops)
        count, nd = {}, 0
        for i in order:
            o = ops[i]
            if o["kind"] == "c":
                count[o["eng"]] = count.get(o["eng"], 0) + 1
                o["sig"] = ("c" + o["eng"], count[o["eng"]])
            elif o["kind"] == "d":
                o["sig"] = ("d%d" % nd, 16)
                nd += 1
            elif o["kind"] == "rx":
                o["sig"] = ("arr%d" % o["fn"], 2 * NENG)
            else:
                count["snt"] = count.get("snt", 0) + 2 * NENG
                o["sig"] = None
        known, waited = {}, {}
        for i in order:
            o = ops[i]
            kn = known.setdefault(o["eng"], {})
            need = {}
            if o["kind"] != "rx":
                for j in o["dep"]:
                    p = ops[j]
                    if p["eng"] == "t" and o["eng"] == "t" and o["acc"]:
                        continue
                    if kn.get(p["sig"][0], 0) < p["sig"][1] and need.get(p["sig"][0], (0, 0))[0] < p["sig"][1]:
                        need[p["sig"][0]] = (p["sig"][1], j)
            for s in list(need):
                if any(s2 != s and ops[need[s2][1]]["clock"].get(s, 0) >= need[s][0] for s2 in need):
                    need.pop(s)
            o["waits"] = [(s, need[s][0]) for s in need]
            for s in need:
                waited[s] = max(waited.get(s, 0), need[s][0])
                for s2, c in ops[need[s][1]]["clock"].items():
                    kn[s2] = max(kn.get(s2, 0), c)
            o["clock"] = dict(kn) if o["kind"] != "rx" else {}
            if o["sig"]:
                o["clock"][o["sig"][0]] = o["sig"][1]
        last = {"snt": count["snt"]}
        for i in order:
            s = ops[i]["sig"]
            if s:
                last[s[0]] = s[1]
        PLAN["ops"], PLAN["order"], PLAN["total"] = ops, order, total
        PLAN["end"] = [(s, c) for s, c in last.items() if waited.get(s, 0) < c]
    return PLAN


def rank_program(g, core, T, topo):
    rank = T.rank_of(core)
    if rank is None:
        return
    p = plan()
    queue = {"g": g, "v": g.vector, "s": g.scalar, "t": g.tensor, "y": g.sync}
    n = len(T.cores)
    for i in p["order"]:
        o = p["ops"][i]
        if o["kind"] == "rx":
            continue
        q = queue[o["eng"]]
        for s, c in o["waits"]:
            q.wait_ge(T.sem[s], c)
        if o["kind"] == "send":
            t, qc, qs, step = o["fn"]
            dst = T.cores[(rank + step) % n]
            assert topo.may_write(core, dst)
            rid, pid = topo.addr(dst)[:2]
            eng = topo.engines(core, dst)
            a, b = 64 + 64 * t, 128 + 64 * t
            g.remote_dma(T.lq[:, a:b].bitcast(dt.uint8), ap(T, qc, dt.uint8), T.sem["arr%d" % t], T.sem.snt, pid, rid, sum(1 << e for e in eng[:NENG]))
            g.remote_dma(T.ls[:, a:b], ap(T, qs), T.sem["arr%d" % t], T.sem.snt, pid, rid, sum(1 << e for e in eng[NENG:2 * NENG]))
        else:
            o["fn"](q, T).then_inc(T.sem[o["sig"][0]], 16 if o["kind"] == "d" else 1)
    for s, c in p["end"]:
        g.wait_ge(T.sem[s], c)
